import numpy as np
import ml_dtypes


def mxq(x, axis, fmt="e4m3"):
    dtype, down = {"e4m3": (ml_dtypes.float8_e4m3fn, 7), "e5m2": (ml_dtypes.float8_e5m2, 14)}[fmt]
    v = np.moveaxis(np.asarray(x, np.float32).astype(ml_dtypes.bfloat16).astype(np.float64), axis, -1)
    blocks = v.reshape(v.shape[:-1] + (-1, 32))
    amax = np.abs(blocks).max(-1, keepdims=True)
    byte = np.maximum(np.where(amax > 0, np.frexp(amax)[1] - 1 + 127, 0) - down, 1)
    scale = np.exp2(byte - 127.0)
    codes = (blocks / scale).astype(np.float32).astype(dtype).astype(np.float64)
    return np.moveaxis((codes * scale).reshape(v.shape), -1, axis)


WIDE = False


def mx_kscale(k):
    if not WIDE:
        return np.ones(k)
    levels = np.array([10, -10, 5, -5, 0])
    if k % 512:
        return np.exp2(np.random.permutation(np.resize(levels, k // 32))).repeat(32)
    a = np.empty((k // 512, 16))
    for p in range(k // 512):
        a[p, :8] = np.random.permutation(np.resize(levels, 8))
        for g in range(8):
            far = levels[np.abs(levels - a[p, g]) >= 10]
            a[p, g + 8] = far[np.random.randint(len(far))]
    return np.exp2(a.ravel()).repeat(32)


def f64(x):
    return np.asarray(x).astype(np.float64)


def striped(idx):
    return np.tile(idx.reshape(-1, 16).T, (8, 1)).astype(np.uint16)


def unstriped(offs):
    return offs[:16].T.reshape(-1).astype(np.int64)


def striped8(idx):
    return np.concatenate([x.reshape(-1, 16).T for x in idx]).astype(np.uint16)


def runs(offs, k):
    lists = np.stack([offs[16 * r : 16 * r + 16].T.reshape(-1) for r in range(8)]).astype(np.int64)
    return lists[np.arange(k) % 512 // 64]


def pack_weight(w):
    k, n = w.shape
    w = f64(np.asarray(w, np.float32).astype(ml_dtypes.bfloat16)).reshape(k // 32, 32, n)
    amax = np.abs(w).max(1)
    byte = np.clip(np.where(amax > 0, np.frexp(amax)[1] - 1 + 127 - 7, 1), 1, 254)
    scaled = (w * np.exp2(127.0 - byte)[:, None, :]).reshape(k, n).astype(np.float32)
    words = np.ascontiguousarray(scaled.reshape(k // 512, 128, 4, n).transpose(0, 1, 3, 2)).astype(ml_dtypes.float8_e4m3fn).view(np.uint8)
    return words, np.ascontiguousarray(byte.astype(np.uint8).reshape(k // 512, 16, n))


def unpack_weight(words, scales):
    g, p, n, _ = words.shape
    vals = np.ascontiguousarray(words).view(ml_dtypes.float8_e4m3fn).astype(np.float64) * np.repeat(np.exp2(scales.astype(np.float64) - 127.0), 8, axis=1)[..., None]
    return vals.transpose(0, 1, 3, 2).reshape(g * 512, n)


def sigmoid(v):
    return 1.0 / (1.0 + np.exp(-np.maximum(v, -700.0)))


K, T, S, V, G, H = 512, 1024, 512, 512, 2048, 512


def setup_inputs():
    n = np.random.standard_normal
    s = mx_kscale(K)[:, None]
    u = mx_kscale(S)
    packed_xT = pack_weight(n((K, T)) * s)
    packed_dT = pack_weight(n((K, G)) / s)
    return {
        "x_words": packed_xT[0],
        "x_scales": packed_xT[1],
        "d_words": packed_dT[0],
        "d_scales": packed_dT[1],
        "w1": (n((K, H)) / np.sqrt(K) / s).astype(np.float32),
        "ga": (np.random.uniform(0.5, 1.5, (H, 1)) * u[:, None]).astype(np.float32),
        "gb": (np.random.uniform(0.5, 1.5, (H, 1)) / u[:, None]).astype(np.float32),
        "offs": striped(np.random.permutation(T)[:S]),
        "k1": striped8(np.random.randint(0, G, (8, H))),
        "two": striped(np.random.permutation(T)[:V]),
        "n1": striped(np.random.permutation(S)),
        "n2": striped(np.random.permutation(S)),
        "n3": striped8(np.stack([np.random.permutation(V) for _ in range(8)])),
        "n4": striped8(np.stack([np.random.permutation(V) for _ in range(8)])),
        "n5": striped(np.random.randint(0, V, G)),
    }


def reference(x_words, x_scales, d_words, d_scales, w1, ga, gb, offs, k1, two, n1, n2, n3, n4, n5):
    d_k1 = unpack_weight(d_words, d_scales)[np.arange(K)[:, None], runs(k1, K)]
    xq = unpack_weight(x_words, x_scales)[:, unstriped(offs)]
    a = 0.0625 * (d_k1.T @ xq)
    z = f64(ga) * (a + (sigmoid(a[:, unstriped(n1)])) * (a[:, unstriped(n2)] - a))
    x_two = unpack_weight(x_words, x_scales)[:, unstriped(two)]
    b = mxq(f64(w1), 0, "e4m3").T @ x_two
    z2 = f64(gb) * (0.75 * ((b - (b[np.arange(H)[:, None], runs(n3, H)])) * (b - (b[np.arange(H)[:, None], runs(n4, H)]))))
    s = 0.0625 * ((mxq(z, 0, "e4m3").T @ mxq(z2, 0, "e4m3")))
    mb = s[:, unstriped(n5)]
    mx = mb.reshape(S, V, 4).max(axis=2)
    mn = mb.reshape(S, V, 4).min(axis=2)
    return np.maximum(np.minimum(1.5 * s, mx), mn)

@@ -1,0 +1,200 @@
+from contextlib import ExitStack
+
+import concourse.mybir as mybir
+
+F32 = mybir.dt.float32
+BF16 = mybir.dt.bfloat16
+I32 = mybir.dt.int32
+U32 = mybir.dt.uint32
+U16 = mybir.dt.uint16
+U8 = mybir.dt.uint8
+FP8X4 = mybir.dt.float8_e4m3fn_x4
+ALU = mybir.AluOpType
+ACT = mybir.ActivationFunctionType
+
+P = 128
+PACK = 4
+N = 512
+T = 1024
+G = 2048
+FLOPS = 3 * 2 * 512 * 512 * 512
+
+A_BLOCKS = [(0, 128), (128, 128), (256, 256)]
+N5_PIECES = {128: [256, 256], 256: [352, 352, 320]}
+
+
+def tile_picked_ckqtrackquadgclip_none_p_kernel(tc, x_words, x_scales, d_words, d_scales, w1, ga, gb, offs, k1, two, n1, n2, n3, n4, n5, out):
+    nc = tc.nc
+    with ExitStack() as ctx:
+        held = ctx.enter_context(tc.tile_pool(name="held", bufs=1))
+        ring = ctx.enter_context(tc.tile_pool(name="ring", bufs=2))
+        psum = ctx.enter_context(tc.psum_pool(name="psum", bufs=1))
+
+        def list_tile(name, src):
+            t = held.tile([P, src.shape[1]], U16, name=name)
+            nc.sync.dma_start(t[:], src)
+            return t
+
+        def entries(lst, start, count):
+            return lst[:, start // 16 : (start + count) // 16]
+
+        ds = held.tile([P, G], U8, name="ds")
+        xs = held.tile([P, T], U8, name="xs")
+        d_rows = d_scales[0].bitcast(I32).rearrange("(g e) c -> e g c", e=2)
+        for e in range(2):
+            nc.gpsimd.dma_start(ds[e:P:2, :].bitcast(I32), d_rows[e].unsqueeze(1).to_broadcast([8, 8, G // 4]))
+
+        two_t = list_tile("two_t", two)
+        k1_t = list_tile("k1_t", k1)
+        x_rows = x_scales[0].bitcast(I32).rearrange("(q j) c -> j q c", j=4)
+        for j in range(4):
+            nc.sync.dma_start(xs[j:P:4, :].bitcast(I32), x_rows[j].unsqueeze(1).to_broadcast([4, 8, T // 4]))
+        w_rows = w1.rearrange("(p j) c -> p j c", j=PACK)
+        w_raw = [held.tile([P, PACK, N // 2], F32, name="w_raw%d" % h) for h in range(2)]
+        for h in range(2):
+            nc.sync.dma_start(w_raw[h][:], w_rows[:, :, h * 256 : (h + 1) * 256])
+        xw = held.tile([P, T], U32, name="xw")
+        nc.sync.dma_start(xw[:].bitcast(I32), x_words[0].rearrange("p c r -> p (c r)").bitcast(I32))
+        offs_t = list_tile("offs_t", offs)
+        dw = held.tile([P, G], U32, name="dw")
+        nc.sync.dma_start(dw[:].bitcast(I32), d_words[0].rearrange("p c r -> p (c r)").bitcast(I32))
+        n3_t = list_tile("n3_t", n3)
+        n4_t = list_tile("n4_t", n4)
+        gb_raw = held.tile([P, PACK], F32, name="gb_raw")
+        nc.sync.dma_start(gb_raw[:], gb.rearrange("(p t) o -> p (t o)", t=PACK))
+        ga_t = held.tile([P, PACK], F32, name="ga_t")
+        nc.sync.dma_start(ga_t[:], ga.rearrange("(p t) o -> p (t o)", t=PACK))
+        n1_t = list_tile("n1_t", n1)
+        n2_t = list_tile("n2_t", n2)
+        n5_t = list_tile("n5_t", n5)
+
+        x2_s = held.tile([P, N], U8, name="x2_s", align_bytes=64)
+        nc.vector.tensor_copy(x2_s[:], xs[:].indirect(two_t[:]))
+        ds_g = held.tile([P, N], U8, name="ds_g", align_bytes=64)
+        nc.vector.tensor_copy(ds_g[:], ds[:].indirect(k1_t[:]))
+        ds_d = held.tile([P, PACK, P], U8, name="ds_d", align_bytes=64)
+        nc.vector.tensor_copy(ds_d[:].rearrange("p t m -> p m t"), ds_g[:].rearrange("p (m t) -> p m t", t=PACK))
+        d_sc = held.tile([P, N], U8, name="d_sc", align_bytes=64)
+        ds_flat = ds_d[:].rearrange("p t m -> p (t m)")
+        nc.vector.tensor_copy(d_sc[:].bitcast(I32), ds_flat.bitcast(I32))
+        for e in range(2):
+            nc.sync.dma_start(d_sc[2 + e : P : 32, :].bitcast(I32), ds_d[16 + e : P : 32, :, :].rearrange("p t m -> p (t m)").bitcast(I32))
+
+        w_bf = held.tile([P, PACK, P, PACK], BF16, name="w_bf", align_bytes=64)
+        for h in range(2):
+            nc.scalar.copy(
+                w_bf[:, :, 64 * h : 64 * (h + 1), :].rearrange("p t m j -> p m j t"),
+                w_raw[h][:].rearrange("p j (m t) -> p m j t", t=PACK),
+            )
+        x2_w = held.tile([P, N], U32, name="x2_w", align_bytes=64)
+        nc.vector.tensor_copy(x2_w[:], xw[:].indirect(two_t[:]))
+        w_w = held.tile([P, PACK, P], U32, name="w_w", align_bytes=64)
+        w_s = held.tile([P, PACK, P], U8, name="w_s", align_bytes=64)
+        b = []
+        for t in range(PACK):
+            nc.vector.quantize_mx(out=w_w[:, t, :].bitcast(FP8X4), scales=w_s[:, t, :], in_=w_bf[:, t, :, :].rearrange("p m j -> p (m j)"))
+            bank = psum.tile([P, N], F32, name="bank_b%d" % t, tag="bank%d" % t)
+            nc.tensor.matmul_mx(out=bank[:], lhsT=w_w[:, t, :].bitcast(FP8X4), lhsT_scale=w_s[:, t, :], rhs=x2_w[:].bitcast(FP8X4), rhs_scale=x2_s[:], start=True, stop=True)
+            b_t = held.tile([P, N], F32, name="b%d" % t)
+            nc.scalar.copy(b_t[:], bank[:])
+            b.append(b_t)
+
+        x1_s = held.tile([P, N], U8, name="x1_s", align_bytes=64)
+        nc.vector.tensor_copy(x1_s[:], xs[:].indirect(offs_t[:]))
+        x1_w = held.tile([P, N], U32, name="x1_w", align_bytes=64)
+        nc.vector.tensor_copy(x1_w[:], xw[:].indirect(offs_t[:]))
+        dw_g = held.tile([P, N], U32, name="dw_g", align_bytes=64)
+        nc.vector.tensor_copy(dw_g[:], dw[:].indirect(k1_t[:]))
+        d_w = held.tile([P, PACK, P], U32, name="d_w", align_bytes=64)
+        nc.vector.tensor_copy(
+            d_w[:].rearrange("p t (c i) -> p c t i", i=4),
+            dw_g[:].rearrange("p (c i t) -> p c t i", i=4, t=PACK),
+        )
+        gb_t = held.tile([P, PACK], F32, name="gb_t")
+        nc.gpsimd.tensor_scalar(gb_t[:], gb_raw[:], 0.75, 0.0, ALU.mult, ALU.add)
+
+        a = []
+        for t in range(PACK):
+            bank = psum.tile([P, N], F32, name="bank_a%d" % t, tag="bank%d" % (4 + t))
+            nc.tensor.matmul_mx(out=bank[:], lhsT=d_w[:, t, :].bitcast(FP8X4), lhsT_scale=d_sc[:, t * P : (t + 1) * P], rhs=x1_w[:].bitcast(FP8X4), rhs_scale=x1_s[:], start=True, stop=True)
+            a_t = held.tile([P, N], F32, name="a%d" % t)
+            nc.vector.tensor_scalar_mul(a_t[:], bank[:], 0.0625)
+            a.append(a_t)
+
+        def quantise(planes, width, name):
+            grouped = held.tile([P, width, PACK], BF16, name=name + "_g", align_bytes=64)
+            nc.vector.tensor_copy(
+                grouped[:].rearrange("p (c i) t -> p c t i", i=4),
+                planes[:].rearrange("p t (c i) -> p c t i", i=4),
+            )
+            words = held.tile([P, width], U32, name=name + "_w", align_bytes=64)
+            scales = held.tile([P, width], U8, name=name + "_s", align_bytes=64)
+            nc.vector.quantize_mx(out=words[:].bitcast(FP8X4), scales=scales[:], in_=grouped[:].rearrange("p c t -> p (c t)"))
+            return words, scales
+
+        z2_planes = held.tile([P, PACK, N], BF16, name="z2_planes")
+        for t in range(PACK):
+            g3 = ring.tile([P, N], F32, name="g3")
+            g4 = ring.tile([P, N], F32, name="g4")
+            for got, lst in ((g3, n3_t), (g4, n4_t)):
+                for h in range(2):
+                    nc.scalar.activation(got[:, h * 256 : (h + 1) * 256], b[t][:].indirect(entries(lst, h * 256, 256)), ACT.Copy)
+            d3 = ring.tile([P, N], F32, name="d3")
+            d4 = ring.tile([P, N], F32, name="d4")
+            nc.vector.tensor_tensor(d3[:], b[t][:], g3[:], ALU.subtract)
+            nc.vector.tensor_tensor(d4[:], b[t][:], g4[:], ALU.subtract)
+            nc.vector.scalar_tensor_tensor(z2_planes[:, t, :], d3[:], gb_t[:, t : t + 1], d4[:], ALU.mult, ALU.mult)
+        z2_w, z2_s = quantise(z2_planes, N, "z2")
+
+        def z_block(start, width):
+            cols = slice(start, start + width)
+            planes = held.tile([P, PACK, width], BF16, name="z_planes%d" % start)
+            sig = held.tile([P, PACK, width], F32, name="sig%d" % start)
+            g2 = held.tile([P, PACK, width], F32, name="g2_%d" % start)
+            d = held.tile([P, PACK, width], F32, name="d_%d" % start)
+            e = held.tile([P, PACK, width], F32, name="e_%d" % start)
+            for t in range(PACK):
+                nc.scalar.activation(g2[:, t, :], a[t][:].indirect(entries(n2_t, start, width)), ACT.Copy)
+                nc.scalar.activation(sig[:, t, :], a[t][:].indirect(entries(n1_t, start, width)), ACT.Sigmoid)
+            for t in range(PACK):
+                nc.vector.tensor_tensor(d[:, t, :], g2[:, t, :], a[t][:, cols], ALU.subtract)
+            for t in range(PACK):
+                nc.vector.scalar_tensor_tensor(e[:, t, :], d[:, t, :], ga_t[:, t : t + 1], sig[:, t, :], ALU.mult, ALU.mult)
+            for t in range(PACK):
+                nc.vector.scalar_tensor_tensor(planes[:, t, :], a[t][:, cols], ga_t[:, t : t + 1], e[:, t, :], ALU.mult, ALU.add)
+            return quantise(planes, width, "z%d" % start)
+
+        def s_rows(row0, z_w, z_s, widths):
+            bank = psum.tile([P, N], F32, name="bank_s%d" % row0, tag="bank%d" % (row0 // P))
+            nc.tensor.matmul_mx(out=bank[:], lhsT=z_w.bitcast(FP8X4), lhsT_scale=z_s, rhs=z2_w[:].bitcast(FP8X4), rhs_scale=z2_s[:], start=True, stop=True)
+            s = held.tile([P, N], F32, name="s%d" % row0)
+            nc.scalar.activation(s[:], bank[:], ACT.Copy, scale=0.0625)
+            v0 = 0
+            for half in widths:
+                mb = ring.tile([P, half, 4], F32, name="mb", bufs=4)
+                flat = mb[:].rearrange("p v m -> p (v m)")
+                at = 0
+                for count in N5_PIECES[half]:
+                    nc.scalar.activation(flat[:, at : at + count], s[:].indirect(entries(n5_t, 4 * v0 + at, count)), ACT.Copy)
+                    at = at + count
+                hi = ring.tile([P, half, 2], F32, name="hi")
+                lo = ring.tile([P, half, 2], F32, name="lo")
+                mx = ring.tile([P, half], F32, name="mx")
+                mn = ring.tile([P, half], F32, name="mn")
+                capped = ring.tile([P, half], F32, name="capped")
+                res = ring.tile([P, half], F32, name="res", bufs=4)
+                nc.vector.tensor_tensor(hi[:], mb[:, :, 0:2], mb[:, :, 2:4], ALU.max)
+                nc.vector.tensor_tensor(lo[:], mb[:, :, 0:2], mb[:, :, 2:4], ALU.min)
+                nc.vector.tensor_tensor(mx[:], hi[:, :, 0], hi[:, :, 1], ALU.max)
+                nc.vector.tensor_tensor(mn[:], lo[:, :, 0], lo[:, :, 1], ALU.min)
+                nc.vector.scalar_tensor_tensor(capped[:], s[:, v0 : v0 + half], 1.5, mx[:], ALU.mult, ALU.min)
+                nc.vector.tensor_tensor(res[:], capped[:], mn[:], ALU.max)
+                nc.sync.dma_start(out[row0 : row0 + P, v0 : v0 + half], res[:])
+                v0 = v0 + half
+
+        blocks = [z_block(start, width) for start, width in A_BLOCKS[:2]]
+        s_rows(0, blocks[0][0][:], blocks[0][1][:], [256, 256])
+        last = z_block(*A_BLOCKS[2])
+        s_rows(128, blocks[1][0][:], blocks[1][1][:], [256, 256])
+        s_rows(256, last[0][:, 0:P], last[1][:, 0:P], [256, 256])
+        s_rows(384, last[0][:, P : 2 * P], last[1][:, P : 2 * P], [256, 128, 128])

@@ -19,8 +19,8 @@ T = 1024
 G = 2048
 FLOPS = 3 * 2 * 512 * 512 * 512
 
-A_BLOCKS = [(0, 128), (128, 128), (256, 256)]
-N5_PIECES = {128: [256, 256], 256: [352, 352, 320]}
+B_WINDOW = 1024
+S_WINDOW = 1056
 
 
 def tile_picked_ckqtrackquadgclip_none_p_kernel(tc, x_words, x_scales, d_words, d_scales, w1, ga, gb, offs, k1, two, n1, n2, n3, n4, n5, out):
@@ -40,26 +40,32 @@ def tile_picked_ckqtrackquadgclip_none_p_kernel(tc, x_words, x_scales, d_words, 
 
         ds = held.tile([P, G], U8, name="ds")
         xs = held.tile([P, T], U8, name="xs")
-        d_rows = d_scales[0].bitcast(I32).rearrange("(g e) c -> e g c", e=2)
-        for e in range(2):
-            nc.gpsimd.dma_start(ds[e:P:2, :].bitcast(I32), d_rows[e].unsqueeze(1).to_broadcast([8, 8, G // 4]))
+        nc.gpsimd.memset(xs[:].bitcast(I32), 0)
+        nc.gpsimd.memset(ds[:].bitcast(I32), 0)
+        b = [held.tile([P, B_WINDOW], F32, name="b%d" % t) for t in range(PACK)]
+        s_tiles = [held.tile([P, S_WINDOW], F32, name="s%d" % t) for t in range(PACK)]
+        for window in b + s_tiles:
+            nc.gpsimd.memset(window[:, N:], 0.0)
 
+        x_rows = x_scales[0].bitcast(I32)
+        for q in range(4):
+            nc.scalar.dma_start(xs[32 * q : 32 * q + 4, :].bitcast(I32), x_rows[4 * q : 4 * q + 4])
         two_t = list_tile("two_t", two)
-        k1_t = list_tile("k1_t", k1)
-        x_rows = x_scales[0].bitcast(I32).rearrange("(q j) c -> j q c", j=4)
-        for j in range(4):
-            nc.sync.dma_start(xs[j:P:4, :].bitcast(I32), x_rows[j].unsqueeze(1).to_broadcast([4, 8, T // 4]))
-        w_rows = w1.rearrange("(p j) c -> p j c", j=PACK)
-        w_raw = [held.tile([P, PACK, N // 2], F32, name="w_raw%d" % h) for h in range(2)]
-        for h in range(2):
-            nc.sync.dma_start(w_raw[h][:], w_rows[:, :, h * 256 : (h + 1) * 256])
+        offs_t = list_tile("offs_t", offs)
         xw = held.tile([P, T], U32, name="xw")
         nc.sync.dma_start(xw[:].bitcast(I32), x_words[0].rearrange("p c r -> p (c r)").bitcast(I32))
-        offs_t = list_tile("offs_t", offs)
-        dw = held.tile([P, G], U32, name="dw")
-        nc.sync.dma_start(dw[:].bitcast(I32), d_words[0].rearrange("p c r -> p (c r)").bitcast(I32))
+        w_rows = w1.rearrange("(p j) c -> p j c", j=PACK)
+        w_raw = [held.tile([P, PACK, N // 2], F32, name="w_raw%d" % h, tag="w_raw%d" % h, align_bytes=64) for h in range(2)]
+        for h in range(2):
+            nc.sync.dma_start(w_raw[h][:], w_rows[:, :, h * 256 : (h + 1) * 256])
+        k1_t = list_tile("k1_t", k1)
+        d_rows = d_scales[0].bitcast(I32).rearrange("(g e) c -> e g c", e=2)
+        for e in range(2):
+            nc.sync.dma_start(ds[e:P:16, :].bitcast(I32), d_rows[e])
         n3_t = list_tile("n3_t", n3)
         n4_t = list_tile("n4_t", n4)
+        dw = held.tile([P, G], U32, name="dw")
+        nc.sync.dma_start(dw[:].bitcast(I32), d_words[0].rearrange("p c r -> p (c r)").bitcast(I32))
         gb_raw = held.tile([P, PACK], F32, name="gb_raw")
         nc.sync.dma_start(gb_raw[:], gb.rearrange("(p t) o -> p (t o)", t=PACK))
         ga_t = held.tile([P, PACK], F32, name="ga_t")
@@ -70,17 +76,9 @@ def tile_picked_ckqtrackquadgclip_none_p_kernel(tc, x_words, x_scales, d_words, 
 
         x2_s = held.tile([P, N], U8, name="x2_s", align_bytes=64)
         nc.vector.tensor_copy(x2_s[:], xs[:].indirect(two_t[:]))
-        ds_g = held.tile([P, N], U8, name="ds_g", align_bytes=64)
-        nc.vector.tensor_copy(ds_g[:], ds[:].indirect(k1_t[:]))
-        ds_d = held.tile([P, PACK, P], U8, name="ds_d", align_bytes=64)
-        nc.vector.tensor_copy(ds_d[:].rearrange("p t m -> p m t"), ds_g[:].rearrange("p (m t) -> p m t", t=PACK))
-        d_sc = held.tile([P, N], U8, name="d_sc", align_bytes=64)
-        ds_flat = ds_d[:].rearrange("p t m -> p (t m)")
-        nc.vector.tensor_copy(d_sc[:].bitcast(I32), ds_flat.bitcast(I32))
-        for e in range(2):
-            nc.sync.dma_start(d_sc[2 + e : P : 32, :].bitcast(I32), ds_d[16 + e : P : 32, :, :].rearrange("p t m -> p (t m)").bitcast(I32))
-
-        w_bf = held.tile([P, PACK, P, PACK], BF16, name="w_bf", align_bytes=64)
+        x1_s = held.tile([P, N], U8, name="x1_s", align_bytes=64)
+        nc.vector.tensor_copy(x1_s[:], xs[:].indirect(offs_t[:]))
+        w_bf = held.tile([P, PACK, P, PACK], BF16, name="w_bf", tag="w_bf", align_bytes=64)
         for h in range(2):
             nc.scalar.copy(
                 w_bf[:, :, 64 * h : 64 * (h + 1), :].rearrange("p t m j -> p m j t"),
@@ -90,18 +88,23 @@ def tile_picked_ckqtrackquadgclip_none_p_kernel(tc, x_words, x_scales, d_words, 
         nc.vector.tensor_copy(x2_w[:], xw[:].indirect(two_t[:]))
         w_w = held.tile([P, PACK, P], U32, name="w_w", align_bytes=64)
         w_s = held.tile([P, PACK, P], U8, name="w_s", align_bytes=64)
-        b = []
         for t in range(PACK):
             nc.vector.quantize_mx(out=w_w[:, t, :].bitcast(FP8X4), scales=w_s[:, t, :], in_=w_bf[:, t, :, :].rearrange("p m j -> p (m j)"))
             bank = psum.tile([P, N], F32, name="bank_b%d" % t, tag="bank%d" % t)
             nc.tensor.matmul_mx(out=bank[:], lhsT=w_w[:, t, :].bitcast(FP8X4), lhsT_scale=w_s[:, t, :], rhs=x2_w[:].bitcast(FP8X4), rhs_scale=x2_s[:], start=True, stop=True)
-            b_t = held.tile([P, N], F32, name="b%d" % t)
-            nc.scalar.copy(b_t[:], bank[:])
-            b.append(b_t)
+            nc.scalar.copy(b[t][:, 0:N], bank[:])
 
-        x1_s = held.tile([P, N], U8, name="x1_s", align_bytes=64)
-        nc.vector.tensor_copy(x1_s[:], xs[:].indirect(offs_t[:]))
-        x1_w = held.tile([P, N], U32, name="x1_w", align_bytes=64)
+        ds_g = held.tile([P, N], U8, name="ds_g", tag="w_raw1", align_bytes=64)
+        nc.vector.tensor_copy(ds_g[:], ds[:].indirect(k1_t[:]))
+        ds_d = held.tile([P, PACK, P], U8, name="ds_d", align_bytes=64)
+        nc.vector.tensor_copy(ds_d[:].rearrange("p t m -> p m t"), ds_g[:].rearrange("p (m t) -> p m t", t=PACK))
+        d_sc = held.tile([P, N], U8, name="d_sc", align_bytes=64)
+        ds_flat = ds_d[:].rearrange("p t m -> p (t m)")
+        nc.vector.tensor_copy(d_sc[:].bitcast(I32), ds_flat.bitcast(I32))
+        for e in range(2):
+            nc.sync.dma_start(d_sc[2 + e : P : 32, :].bitcast(I32), ds_d[16 + e : P : 32, :, :].rearrange("p t m -> p (t m)").bitcast(I32))
+
+        x1_w = held.tile([P, N], U32, name="x1_w", tag="w_bf", align_bytes=64)
         nc.vector.tensor_copy(x1_w[:], xw[:].indirect(offs_t[:]))
         dw_g = held.tile([P, N], U32, name="dw_g", align_bytes=64)
         nc.vector.tensor_copy(dw_g[:], dw[:].indirect(k1_t[:]))
@@ -137,12 +140,11 @@ def tile_picked_ckqtrackquadgclip_none_p_kernel(tc, x_words, x_scales, d_words, 
             g3 = ring.tile([P, N], F32, name="g3")
             g4 = ring.tile([P, N], F32, name="g4")
             for got, lst in ((g3, n3_t), (g4, n4_t)):
-                for h in range(2):
-                    nc.scalar.activation(got[:, h * 256 : (h + 1) * 256], b[t][:].indirect(entries(lst, h * 256, 256)), ACT.Copy)
+                nc.scalar.activation(got[:], b[t][:].indirect(lst[:]), ACT.Copy)
             d3 = ring.tile([P, N], F32, name="d3")
             d4 = ring.tile([P, N], F32, name="d4")
-            nc.vector.tensor_tensor(d3[:], b[t][:], g3[:], ALU.subtract)
-            nc.vector.tensor_tensor(d4[:], b[t][:], g4[:], ALU.subtract)
+            nc.vector.tensor_tensor(d3[:], b[t][:, 0:N], g3[:], ALU.subtract)
+            nc.vector.tensor_tensor(d4[:], b[t][:, 0:N], g4[:], ALU.subtract)
             nc.vector.scalar_tensor_tensor(z2_planes[:, t, :], d3[:], gb_t[:, t : t + 1], d4[:], ALU.mult, ALU.mult)
         z2_w, z2_s = quantise(z2_planes, N, "z2")
 
@@ -167,16 +169,12 @@ def tile_picked_ckqtrackquadgclip_none_p_kernel(tc, x_words, x_scales, d_words, 
         def s_rows(row0, z_w, z_s, widths):
             bank = psum.tile([P, N], F32, name="bank_s%d" % row0, tag="bank%d" % (row0 // P))
             nc.tensor.matmul_mx(out=bank[:], lhsT=z_w.bitcast(FP8X4), lhsT_scale=z_s, rhs=z2_w[:].bitcast(FP8X4), rhs_scale=z2_s[:], start=True, stop=True)
-            s = held.tile([P, N], F32, name="s%d" % row0)
-            nc.scalar.activation(s[:], bank[:], ACT.Copy, scale=0.0625)
+            s = s_tiles[row0 // P]
+            nc.scalar.activation(s[:, 0:N], bank[:], ACT.Copy, scale=0.0625)
             v0 = 0
             for half in widths:
                 mb = ring.tile([P, half, 4], F32, name="mb", bufs=4)
-                flat = mb[:].rearrange("p v m -> p (v m)")
-                at = 0
-                for count in N5_PIECES[half]:
-                    nc.scalar.activation(flat[:, at : at + count], s[:].indirect(entries(n5_t, 4 * v0 + at, count)), ACT.Copy)
-                    at = at + count
+                nc.scalar.activation(mb[:].rearrange("p v m -> p (v m)"), s[:].indirect(entries(n5_t, 4 * v0, 4 * half)), ACT.Copy)
                 hi = ring.tile([P, half, 2], F32, name="hi")
                 lo = ring.tile([P, half, 2], F32, name="lo")
                 mx = ring.tile([P, half], F32, name="mx")
@@ -192,9 +190,9 @@ def tile_picked_ckqtrackquadgclip_none_p_kernel(tc, x_words, x_scales, d_words, 
                 nc.sync.dma_start(out[row0 : row0 + P, v0 : v0 + half], res[:])
                 v0 = v0 + half
 
-        blocks = [z_block(start, width) for start, width in A_BLOCKS[:2]]
-        s_rows(0, blocks[0][0][:], blocks[0][1][:], [256, 256])
-        last = z_block(*A_BLOCKS[2])
-        s_rows(128, blocks[1][0][:], blocks[1][1][:], [256, 256])
-        s_rows(256, last[0][:, 0:P], last[1][:, 0:P], [256, 256])
-        s_rows(384, last[0][:, P : 2 * P], last[1][:, P : 2 * P], [256, 128, 128])
+        first = z_block(0, 256)
+        second = z_block(256, 256)
+        s_rows(0, first[0][:, 0:P], first[1][:, 0:P], [256, 256])
+        s_rows(128, first[0][:, P : 2 * P], first[1][:, P : 2 * P], [256, 256])
+        s_rows(256, second[0][:, 0:P], second[1][:, 0:P], [256, 256])
+        s_rows(384, second[0][:, P : 2 * P], second[1][:, P : 2 * P], [256, 128, 128])

@@ -15,12 +15,14 @@ ACT = mybir.ActivationFunctionType
 P = 128
 PACK = 4
 N = 512
-T = 1024
-G = 2048
-FLOPS = 3 * 2 * 512 * 512 * 512
-
-B_WINDOW = 1024
-S_WINDOW = 1056
+HALF = N // 2
+TOKENS = 1024
+CODEWORDS = 2048
+MEMBERS = 4
+SIXTEENTH = 0.0625
+B_COLUMNS = 2 * N
+S_COLUMNS = MEMBERS * HALF + 32
+FLOPS = 3 * 2 * N * N * N
 
 
 def tile_picked_ckqtrackquadgclip_none_p_kernel(tc, x_words, x_scales, d_words, d_scales, w1, ga, gb, offs, k1, two, n1, n2, n3, n4, n5, out):
@@ -30,169 +32,203 @@ def tile_picked_ckqtrackquadgclip_none_p_kernel(tc, x_words, x_scales, d_words, 
         ring = ctx.enter_context(tc.tile_pool(name="ring", bufs=2))
         psum = ctx.enter_context(tc.psum_pool(name="psum", bufs=1))
 
-        def list_tile(name, src):
-            t = held.tile([P, src.shape[1]], U16, name=name)
-            nc.sync.dma_start(t[:], src)
-            return t
+        def load_list(name, src):
+            tile = held.tile([P, src.shape[1]], U16, name=name)
+            nc.sync.dma_start(tile[:], src)
+            return tile
 
-        def entries(lst, start, count):
-            return lst[:, start // 16 : (start + count) // 16]
+        def entries(tile, start, count):
+            return tile[:, start // 16 : (start + count) // 16]
 
-        ds = held.tile([P, G], U8, name="ds")
-        xs = held.tile([P, T], U8, name="xs")
-        nc.gpsimd.memset(xs[:].bitcast(I32), 0)
-        nc.gpsimd.memset(ds[:].bitcast(I32), 0)
-        b = [held.tile([P, B_WINDOW], F32, name="b%d" % t) for t in range(PACK)]
-        s_tiles = [held.tile([P, S_WINDOW], F32, name="s%d" % t) for t in range(PACK)]
-        for window in b + s_tiles:
-            nc.gpsimd.memset(window[:, N:], 0.0)
+        def product(name, bank_number, lhs_words, lhs_scales, rhs_words, rhs_scales):
+            bank = psum.tile([P, N], F32, name=name, tag="bank%d" % bank_number)
+            nc.tensor.matmul_mx(
+                out=bank[:],
+                lhsT=lhs_words.bitcast(FP8X4),
+                lhsT_scale=lhs_scales,
+                rhs=rhs_words.bitcast(FP8X4),
+                rhs_scale=rhs_scales,
+                start=True,
+                stop=True,
+            )
+            return bank
+
+        x_table_scales = held.tile([P, TOKENS], U8, name="x_table_scales")
+        d_table_scales = held.tile([P, CODEWORDS], U8, name="d_table_scales")
+        nc.gpsimd.memset(x_table_scales[:].bitcast(I32), 0)
+        warm_in = held.tile([P, 1], F32, name="warm_in")
+        nc.gpsimd.memset(warm_in[:], 0.0)
+        nc.gpsimd.memset(d_table_scales[:].bitcast(I32), 0)
+        b = [held.tile([P, B_COLUMNS], F32, name="b%d" % t) for t in range(PACK)]
+        s = [held.tile([P, S_COLUMNS], F32, name="s%d" % r) for r in range(PACK)]
+        for tile in b + s:
+            nc.gpsimd.memset(tile[:, N:], 0.0)
 
         x_rows = x_scales[0].bitcast(I32)
         for q in range(4):
-            nc.scalar.dma_start(xs[32 * q : 32 * q + 4, :].bitcast(I32), x_rows[4 * q : 4 * q + 4])
-        two_t = list_tile("two_t", two)
-        offs_t = list_tile("offs_t", offs)
-        xw = held.tile([P, T], U32, name="xw")
-        nc.sync.dma_start(xw[:].bitcast(I32), x_words[0].rearrange("p c r -> p (c r)").bitcast(I32))
+            nc.scalar.dma_start(x_table_scales[32 * q : 32 * q + 4, :].bitcast(I32), x_rows[4 * q : 4 * q + 4])
+        warm = held.tile([P, 1], F32, name="warm")
+        nc.scalar.activation(warm[:], warm_in[:], ACT.Sigmoid)
+        two_list = load_list("two_list", two)
+        offs_list = load_list("offs_list", offs)
+        x_table = held.tile([P, TOKENS], U32, name="x_table")
+        nc.sync.dma_start(x_table[:].bitcast(I32), x_words[0].rearrange("p c r -> p (c r)").bitcast(I32))
         w_rows = w1.rearrange("(p j) c -> p j c", j=PACK)
-        w_raw = [held.tile([P, PACK, N // 2], F32, name="w_raw%d" % h, tag="w_raw%d" % h, align_bytes=64) for h in range(2)]
+        w_raw = [held.tile([P, PACK, HALF], F32, name="w_raw%d" % h, tag="w_raw%d" % h, align_bytes=64) for h in range(2)]
         for h in range(2):
-            nc.sync.dma_start(w_raw[h][:], w_rows[:, :, h * 256 : (h + 1) * 256])
-        k1_t = list_tile("k1_t", k1)
+            nc.sync.dma_start(w_raw[h][:], w_rows[:, :, h * HALF : (h + 1) * HALF])
+        k1_list = load_list("k1_list", k1)
         d_rows = d_scales[0].bitcast(I32).rearrange("(g e) c -> e g c", e=2)
         for e in range(2):
-            nc.sync.dma_start(ds[e:P:16, :].bitcast(I32), d_rows[e])
-        n3_t = list_tile("n3_t", n3)
-        n4_t = list_tile("n4_t", n4)
-        dw = held.tile([P, G], U32, name="dw")
-        nc.sync.dma_start(dw[:].bitcast(I32), d_words[0].rearrange("p c r -> p (c r)").bitcast(I32))
+            nc.sync.dma_start(d_table_scales[e:P:16, :].bitcast(I32), d_rows[e])
+        d_table = held.tile([P, CODEWORDS], U32, name="d_table")
+        nc.sync.dma_start(d_table[:].bitcast(I32), d_words[0].rearrange("p c r -> p (c r)").bitcast(I32))
+        n3_list = load_list("n3_list", n3)
+        n4_list = load_list("n4_list", n4)
         gb_raw = held.tile([P, PACK], F32, name="gb_raw")
         nc.sync.dma_start(gb_raw[:], gb.rearrange("(p t) o -> p (t o)", t=PACK))
-        ga_t = held.tile([P, PACK], F32, name="ga_t")
-        nc.sync.dma_start(ga_t[:], ga.rearrange("(p t) o -> p (t o)", t=PACK))
-        n1_t = list_tile("n1_t", n1)
-        n2_t = list_tile("n2_t", n2)
-        n5_t = list_tile("n5_t", n5)
+        ga_raw = held.tile([P, PACK], F32, name="ga_raw")
+        nc.sync.dma_start(ga_raw[:], ga.rearrange("(p t) o -> p (t o)", t=PACK))
+        n2_list = load_list("n2_list", n2)
+        n1_list = load_list("n1_list", n1)
+        n5_list = load_list("n5_list", n5)
 
-        x2_s = held.tile([P, N], U8, name="x2_s", align_bytes=64)
-        nc.vector.tensor_copy(x2_s[:], xs[:].indirect(two_t[:]))
-        x1_s = held.tile([P, N], U8, name="x1_s", align_bytes=64)
-        nc.vector.tensor_copy(x1_s[:], xs[:].indirect(offs_t[:]))
-        w_bf = held.tile([P, PACK, P, PACK], BF16, name="w_bf", tag="w_bf", align_bytes=64)
+        two_words = held.tile([P, N], U32, name="two_words", align_bytes=64)
+        nc.vector.tensor_copy(two_words[:], x_table[:].indirect(two_list[:]))
+        two_scales = held.tile([P, N], U8, name="two_scales", align_bytes=64)
+        nc.vector.tensor_copy(two_scales[:], x_table_scales[:].indirect(two_list[:]))
+        offs_scales = held.tile([P, N], U8, name="offs_scales", align_bytes=64)
+        nc.vector.tensor_copy(offs_scales[:], x_table_scales[:].indirect(offs_list[:]))
+
+        w_grouped = held.tile([P, PACK, P, PACK], BF16, name="w_grouped", tag="w_grouped", align_bytes=64)
         for h in range(2):
             nc.scalar.copy(
-                w_bf[:, :, 64 * h : 64 * (h + 1), :].rearrange("p t m j -> p m j t"),
+                w_grouped[:, :, h * P // 2 : (h + 1) * P // 2, :].rearrange("p t m j -> p m j t"),
                 w_raw[h][:].rearrange("p j (m t) -> p m j t", t=PACK),
             )
-        x2_w = held.tile([P, N], U32, name="x2_w", align_bytes=64)
-        nc.vector.tensor_copy(x2_w[:], xw[:].indirect(two_t[:]))
-        w_w = held.tile([P, PACK, P], U32, name="w_w", align_bytes=64)
-        w_s = held.tile([P, PACK, P], U8, name="w_s", align_bytes=64)
+        w_words = held.tile([P, PACK, P], U32, name="w_words", align_bytes=64)
+        w_scales = held.tile([P, PACK, P], U8, name="w_scales", align_bytes=64)
+        b_banks = []
         for t in range(PACK):
-            nc.vector.quantize_mx(out=w_w[:, t, :].bitcast(FP8X4), scales=w_s[:, t, :], in_=w_bf[:, t, :, :].rearrange("p m j -> p (m j)"))
-            bank = psum.tile([P, N], F32, name="bank_b%d" % t, tag="bank%d" % t)
-            nc.tensor.matmul_mx(out=bank[:], lhsT=w_w[:, t, :].bitcast(FP8X4), lhsT_scale=w_s[:, t, :], rhs=x2_w[:].bitcast(FP8X4), rhs_scale=x2_s[:], start=True, stop=True)
-            nc.scalar.copy(b[t][:, 0:N], bank[:])
+            nc.vector.quantize_mx(
+                out=w_words[:, t, :].bitcast(FP8X4),
+                scales=w_scales[:, t, :],
+                in_=w_grouped[:, t, :, :].rearrange("p m j -> p (m j)"),
+            )
+            b_banks.append(product("b_bank%d" % t, t, w_words[:, t, :], w_scales[:, t, :], two_words[:], two_scales[:]))
+        nc.scalar.copy(b[0][:, 0:N], b_banks[0][:])
 
-        ds_g = held.tile([P, N], U8, name="ds_g", tag="w_raw1", align_bytes=64)
-        nc.vector.tensor_copy(ds_g[:], ds[:].indirect(k1_t[:]))
-        ds_d = held.tile([P, PACK, P], U8, name="ds_d", align_bytes=64)
-        nc.vector.tensor_copy(ds_d[:].rearrange("p t m -> p m t"), ds_g[:].rearrange("p (m t) -> p m t", t=PACK))
-        d_sc = held.tile([P, N], U8, name="d_sc", align_bytes=64)
-        ds_flat = ds_d[:].rearrange("p t m -> p (t m)")
-        nc.vector.tensor_copy(d_sc[:].bitcast(I32), ds_flat.bitcast(I32))
+        k1_scales = held.tile([P, N], U8, name="k1_scales", tag="w_raw1", align_bytes=64)
+        nc.vector.tensor_copy(k1_scales[:], d_table_scales[:].indirect(k1_list[:]))
+        picked_order = k1_scales[:].rearrange("p (m t) -> p m t", t=PACK)
+        d_mm_scales = held.tile([P, N], U8, name="d_mm_scales", align_bytes=64)
+        nc.vector.tensor_copy(d_mm_scales[:].rearrange("p (t m) -> p m t", t=PACK), picked_order)
         for e in range(2):
-            nc.sync.dma_start(d_sc[2 + e : P : 32, :].bitcast(I32), ds_d[16 + e : P : 32, :, :].rearrange("p t m -> p (t m)").bitcast(I32))
+            nc.sync.dma_start(d_mm_scales[2 + e : P : 32, :].bitcast(I32), d_mm_scales[16 + e : P : 32, :].bitcast(I32))
 
-        x1_w = held.tile([P, N], U32, name="x1_w", tag="w_bf", align_bytes=64)
-        nc.vector.tensor_copy(x1_w[:], xw[:].indirect(offs_t[:]))
-        dw_g = held.tile([P, N], U32, name="dw_g", align_bytes=64)
-        nc.vector.tensor_copy(dw_g[:], dw[:].indirect(k1_t[:]))
-        d_w = held.tile([P, PACK, P], U32, name="d_w", align_bytes=64)
+        offs_words = held.tile([P, N], U32, name="offs_words", tag="w_grouped", align_bytes=64)
+        nc.vector.tensor_copy(offs_words[:], x_table[:].indirect(offs_list[:]))
+        k1_words = held.tile([P, N], U32, name="k1_words", tag="k1_words")
+        nc.vector.tensor_copy(k1_words[:], d_table[:].indirect(k1_list[:]))
+        d_mm_words = held.tile([P, PACK, P], U32, name="d_mm_words", align_bytes=64)
         nc.vector.tensor_copy(
-            d_w[:].rearrange("p t (c i) -> p c t i", i=4),
-            dw_g[:].rearrange("p (c i t) -> p c t i", i=4, t=PACK),
+            d_mm_words[:].rearrange("p t (c i) -> p c t i", i=4),
+            k1_words[:].rearrange("p (c i t) -> p c t i", i=4, t=PACK),
         )
-        gb_t = held.tile([P, PACK], F32, name="gb_t")
-        nc.gpsimd.tensor_scalar(gb_t[:], gb_raw[:], 0.75, 0.0, ALU.mult, ALU.add)
+        for t in range(1, PACK):
+            nc.vector.tensor_copy(b[t][:, 0:N], b_banks[t][:])
+
+        gb_weight = held.tile([P, PACK], F32, name="gb_weight")
+        nc.gpsimd.tensor_scalar(gb_weight[:], gb_raw[:], 0.75, 0.0, ALU.mult, ALU.add)
+        ga_sixteenth = held.tile([P, PACK], F32, name="ga_sixteenth")
+        nc.gpsimd.tensor_scalar(ga_sixteenth[:], ga_raw[:], SIXTEENTH, 0.0, ALU.mult, ALU.add)
 
         a = []
+        a_banks = []
         for t in range(PACK):
-            bank = psum.tile([P, N], F32, name="bank_a%d" % t, tag="bank%d" % (4 + t))
-            nc.tensor.matmul_mx(out=bank[:], lhsT=d_w[:, t, :].bitcast(FP8X4), lhsT_scale=d_sc[:, t * P : (t + 1) * P], rhs=x1_w[:].bitcast(FP8X4), rhs_scale=x1_s[:], start=True, stop=True)
-            a_t = held.tile([P, N], F32, name="a%d" % t)
-            nc.vector.tensor_scalar_mul(a_t[:], bank[:], 0.0625)
-            a.append(a_t)
+            bank = product("a_bank%d" % t, PACK + t, d_mm_words[:, t, :], d_mm_scales[:, t * P : (t + 1) * P], offs_words[:], offs_scales[:])
+            a_tile = held.tile([P, N], F32, name="a%d" % t)
+            nc.vector.tensor_scalar_mul(a_tile[:], bank[:], SIXTEENTH)
+            a.append(a_tile)
+            a_banks.append(bank)
 
-        def quantise(planes, width, name):
-            grouped = held.tile([P, width, PACK], BF16, name=name + "_g", align_bytes=64)
+        def quantise(name, planes, width):
+            grouped = held.tile([P, width, PACK], BF16, name=name + "_grouped", align_bytes=64)
             nc.vector.tensor_copy(
                 grouped[:].rearrange("p (c i) t -> p c t i", i=4),
                 planes[:].rearrange("p t (c i) -> p c t i", i=4),
             )
-            words = held.tile([P, width], U32, name=name + "_w", align_bytes=64)
-            scales = held.tile([P, width], U8, name=name + "_s", align_bytes=64)
+            words = held.tile([P, width], U32, name=name + "_words", align_bytes=64)
+            scales = held.tile([P, width], U8, name=name + "_scales", align_bytes=64)
             nc.vector.quantize_mx(out=words[:].bitcast(FP8X4), scales=scales[:], in_=grouped[:].rearrange("p c t -> p (c t)"))
             return words, scales
 
+        b_diffs = [
+            held.tile([P, 2, 2, N], F32, name="b_diffs0", tag="k1_words"),
+            held.tile([P, 2, 2, N], F32, name="b_diffs1", tag="w_grouped", align_bytes=64),
+        ]
         z2_planes = held.tile([P, PACK, N], BF16, name="z2_planes")
         for t in range(PACK):
-            g3 = ring.tile([P, N], F32, name="g3")
-            g4 = ring.tile([P, N], F32, name="g4")
-            for got, lst in ((g3, n3_t), (g4, n4_t)):
-                nc.scalar.activation(got[:], b[t][:].indirect(lst[:]), ACT.Copy)
-            d3 = ring.tile([P, N], F32, name="d3")
-            d4 = ring.tile([P, N], F32, name="d4")
-            nc.vector.tensor_tensor(d3[:], b[t][:, 0:N], g3[:], ALU.subtract)
-            nc.vector.tensor_tensor(d4[:], b[t][:, 0:N], g4[:], ALU.subtract)
-            nc.vector.scalar_tensor_tensor(z2_planes[:, t, :], d3[:], gb_t[:, t : t + 1], d4[:], ALU.mult, ALU.mult)
-        z2_w, z2_s = quantise(z2_planes, N, "z2")
+            b_n3 = ring.tile([P, N], F32, name="b_n3", bufs=PACK)
+            b_n4 = ring.tile([P, N], F32, name="b_n4", bufs=PACK)
+            nc.scalar.activation(b_n3[:], b[t][:].indirect(n3_list[:]), ACT.Copy)
+            nc.scalar.activation(b_n4[:], b[t][:].indirect(n4_list[:]), ACT.Copy)
+            diff3 = b_diffs[t // 2][:, t % 2, 0, :]
+            diff4 = b_diffs[t // 2][:, t % 2, 1, :]
+            nc.vector.tensor_tensor(diff3, b_banks[t][:], b_n3[:], ALU.subtract)
+            nc.vector.tensor_tensor(diff4, b_banks[t][:], b_n4[:], ALU.subtract)
+            if t < PACK - 1:
+                diff3_weighted = ring.tile([P, N], F32, name="diff3_weighted")
+                nc.gpsimd.tensor_scalar(diff3_weighted[:], diff3, gb_weight[:, t : t + 1], 0.0, ALU.mult, ALU.add)
+                nc.gpsimd.tensor_tensor(z2_planes[:, t, :], diff3_weighted[:], diff4, ALU.mult)
+            else:
+                nc.vector.scalar_tensor_tensor(z2_planes[:, t, :], diff3, gb_weight[:, t : t + 1], diff4, ALU.mult, ALU.mult)
+        z2_words, z2_scales = quantise("z2", z2_planes, N)
 
-        def z_block(start, width):
-            cols = slice(start, start + width)
-            planes = held.tile([P, PACK, width], BF16, name="z_planes%d" % start)
-            sig = held.tile([P, PACK, width], F32, name="sig%d" % start)
-            g2 = held.tile([P, PACK, width], F32, name="g2_%d" % start)
-            d = held.tile([P, PACK, width], F32, name="d_%d" % start)
-            e = held.tile([P, PACK, width], F32, name="e_%d" % start)
+        def z_half(h):
+            cols = slice(h * HALF, (h + 1) * HALF)
+            planes = held.tile([P, PACK, HALF], BF16, name="z_planes%d" % h, tag="z_stage%d" % (h + 1))
+            sig = held.tile([P, PACK, HALF], F32, name="sig%d" % h)
+            a_n2 = held.tile([P, PACK, HALF], F32, name="a_n2_%d" % h)
+            diff = held.tile([P, PACK, HALF], F32, name="diff_%d" % h, tag="z_stage%d" % h)
+            pull = held.tile([P, PACK, HALF], F32, name="pull%d" % h)
             for t in range(PACK):
-                nc.scalar.activation(g2[:, t, :], a[t][:].indirect(entries(n2_t, start, width)), ACT.Copy)
-                nc.scalar.activation(sig[:, t, :], a[t][:].indirect(entries(n1_t, start, width)), ACT.Sigmoid)
+                nc.scalar.activation(a_n2[:, t, :], a[t][:].indirect(entries(n2_list, h * HALF, HALF)), ACT.Copy)
             for t in range(PACK):
-                nc.vector.tensor_tensor(d[:, t, :], g2[:, t, :], a[t][:, cols], ALU.subtract)
+                nc.scalar.activation(sig[:, t, :], a[t][:].indirect(entries(n1_list, h * HALF, HALF)), ACT.Sigmoid)
             for t in range(PACK):
-                nc.vector.scalar_tensor_tensor(e[:, t, :], d[:, t, :], ga_t[:, t : t + 1], sig[:, t, :], ALU.mult, ALU.mult)
+                nc.vector.scalar_tensor_tensor(diff[:, t, :], a_banks[t][:, cols], SIXTEENTH, a_n2[:, t, :], ALU.mult, ALU.subtract)
             for t in range(PACK):
-                nc.vector.scalar_tensor_tensor(planes[:, t, :], a[t][:, cols], ga_t[:, t : t + 1], e[:, t, :], ALU.mult, ALU.add)
-            return quantise(planes, width, "z%d" % start)
+                nc.vector.scalar_tensor_tensor(pull[:, t, :], diff[:, t, :], ga_raw[:, t : t + 1], sig[:, t, :], ALU.mult, ALU.mult)
+            for t in range(PACK):
+                nc.vector.scalar_tensor_tensor(planes[:, t, :], a_banks[t][:, cols], ga_sixteenth[:, t : t + 1], pull[:, t, :], ALU.mult, ALU.subtract)
+            return quantise("z%d" % h, planes, HALF)
 
-        def s_rows(row0, z_w, z_s, widths):
-            bank = psum.tile([P, N], F32, name="bank_s%d" % row0, tag="bank%d" % (row0 // P))
-            nc.tensor.matmul_mx(out=bank[:], lhsT=z_w.bitcast(FP8X4), lhsT_scale=z_s, rhs=z2_w[:].bitcast(FP8X4), rhs_scale=z2_s[:], start=True, stop=True)
-            s = s_tiles[row0 // P]
-            nc.scalar.activation(s[:, 0:N], bank[:], ACT.Copy, scale=0.0625)
-            v0 = 0
-            for half in widths:
-                mb = ring.tile([P, half, 4], F32, name="mb", bufs=4)
-                nc.scalar.activation(mb[:].rearrange("p v m -> p (v m)"), s[:].indirect(entries(n5_t, 4 * v0, 4 * half)), ACT.Copy)
-                hi = ring.tile([P, half, 2], F32, name="hi")
-                lo = ring.tile([P, half, 2], F32, name="lo")
-                mx = ring.tile([P, half], F32, name="mx")
-                mn = ring.tile([P, half], F32, name="mn")
-                capped = ring.tile([P, half], F32, name="capped")
-                res = ring.tile([P, half], F32, name="res", bufs=4)
-                nc.vector.tensor_tensor(hi[:], mb[:, :, 0:2], mb[:, :, 2:4], ALU.max)
-                nc.vector.tensor_tensor(lo[:], mb[:, :, 0:2], mb[:, :, 2:4], ALU.min)
-                nc.vector.tensor_tensor(mx[:], hi[:, :, 0], hi[:, :, 1], ALU.max)
-                nc.vector.tensor_tensor(mn[:], lo[:, :, 0], lo[:, :, 1], ALU.min)
-                nc.vector.scalar_tensor_tensor(capped[:], s[:, v0 : v0 + half], 1.5, mx[:], ALU.mult, ALU.min)
-                nc.vector.tensor_tensor(res[:], capped[:], mn[:], ALU.max)
-                nc.sync.dma_start(out[row0 : row0 + P, v0 : v0 + half], res[:])
-                v0 = v0 + half
+        z_halves = [z_half(h) for h in range(2)]
 
-        first = z_block(0, 256)
-        second = z_block(256, 256)
-        s_rows(0, first[0][:, 0:P], first[1][:, 0:P], [256, 256])
-        s_rows(128, first[0][:, P : 2 * P], first[1][:, P : 2 * P], [256, 256])
-        s_rows(256, second[0][:, 0:P], second[1][:, 0:P], [256, 256])
-        s_rows(384, second[0][:, P : 2 * P], second[1][:, P : 2 * P], [256, 128, 128])
+        for r in range(PACK):
+            z_words, z_scales = z_halves[r // 2]
+            z_cols = slice(r % 2 * P, (r % 2 + 1) * P)
+            bank = product("s_bank%d" % r, r, z_words[:, z_cols], z_scales[:, z_cols], z2_words[:], z2_scales[:])
+            nc.scalar.activation(s[r][:, 0:N], bank[:], ACT.Copy, scale=SIXTEENTH)
+            for h in range(2):
+                cols = slice(h * HALF, (h + 1) * HALF)
+                members = ring.tile([P, HALF, MEMBERS], F32, name="members", bufs=4)
+                nc.scalar.activation(
+                    members[:].rearrange("p v m -> p (v m)"),
+                    s[r][:].indirect(entries(n5_list, h * HALF * MEMBERS, HALF * MEMBERS)),
+                    ACT.Copy,
+                )
+                high_pair = ring.tile([P, HALF, 2], F32, name="high_pair")
+                low_pair = ring.tile([P, HALF, 2], F32, name="low_pair")
+                largest = ring.tile([P, HALF], F32, name="largest")
+                smallest = ring.tile([P, HALF], F32, name="smallest")
+                capped = ring.tile([P, HALF], F32, name="capped")
+                result = ring.tile([P, HALF], F32, name="result", bufs=4)
+                nc.vector.tensor_tensor(high_pair[:], members[:, :, 0:2], members[:, :, 2:4], ALU.max)
+                nc.vector.tensor_tensor(low_pair[:], members[:, :, 0:2], members[:, :, 2:4], ALU.min)
+                nc.vector.tensor_tensor(largest[:], high_pair[:, :, 0], high_pair[:, :, 1], ALU.max)
+                nc.vector.tensor_tensor(smallest[:], low_pair[:, :, 0], low_pair[:, :, 1], ALU.min)
+                nc.vector.scalar_tensor_tensor(capped[:], s[r][:, cols], 1.5, largest[:], ALU.mult, ALU.min)
+                nc.vector.tensor_tensor(result[:], capped[:], smallest[:], ALU.max)
+                nc.sync.dma_start(out[r * P : (r + 1) * P, cols], result[:])

from contextlib import ExitStack

import concourse.mybir as mybir

F32 = mybir.dt.float32
BF16 = mybir.dt.bfloat16
I32 = mybir.dt.int32
U32 = mybir.dt.uint32
U16 = mybir.dt.uint16
U8 = mybir.dt.uint8
FP8X4 = mybir.dt.float8_e4m3fn_x4
ALU = mybir.AluOpType
ACT = mybir.ActivationFunctionType

P = 128
PACK = 4
N = 512
HALF = N // 2
TOKENS = 1024
CODEWORDS = 2048
MEMBERS = 4
SIXTEENTH = 0.0625
B_COLUMNS = 2 * N
S_COLUMNS = MEMBERS * HALF + 32
FLOPS = 3 * 2 * N * N * N


def tile_picked_ckqtrackquadgclip_none_p_kernel(tc, x_words, x_scales, d_words, d_scales, w1, ga, gb, offs, k1, two, n1, n2, n3, n4, n5, out):
    nc = tc.nc
    with ExitStack() as ctx:
        held = ctx.enter_context(tc.tile_pool(name="held", bufs=1))
        ring = ctx.enter_context(tc.tile_pool(name="ring", bufs=2))
        psum = ctx.enter_context(tc.psum_pool(name="psum", bufs=1))

        def load_list(name, src):
            tile = held.tile([P, src.shape[1]], U16, name=name)
            nc.sync.dma_start(tile[:], src)
            return tile

        def entries(tile, start, count):
            return tile[:, start // 16 : (start + count) // 16]

        def product(name, bank_number, lhs_words, lhs_scales, rhs_words, rhs_scales):
            bank = psum.tile([P, N], F32, name=name, tag="bank%d" % bank_number)
            nc.tensor.matmul_mx(
                out=bank[:],
                lhsT=lhs_words.bitcast(FP8X4),
                lhsT_scale=lhs_scales,
                rhs=rhs_words.bitcast(FP8X4),
                rhs_scale=rhs_scales,
                start=True,
                stop=True,
            )
            return bank

        x_table_scales = held.tile([P, TOKENS], U8, name="x_table_scales")
        d_table_scales = held.tile([P, CODEWORDS], U8, name="d_table_scales")
        nc.gpsimd.memset(x_table_scales[:].bitcast(I32), 0)
        warm_in = held.tile([P, 1], F32, name="warm_in")
        nc.gpsimd.memset(warm_in[:], 0.0)
        nc.gpsimd.memset(d_table_scales[:].bitcast(I32), 0)
        b = [held.tile([P, B_COLUMNS], F32, name="b%d" % t) for t in range(PACK)]
        s = [held.tile([P, S_COLUMNS], F32, name="s%d" % r) for r in range(PACK)]
        for tile in b + s:
            nc.gpsimd.memset(tile[:, N:], 0.0)

        x_rows = x_scales[0].bitcast(I32)
        for q in range(4):
            nc.scalar.dma_start(x_table_scales[32 * q : 32 * q + 4, :].bitcast(I32), x_rows[4 * q : 4 * q + 4])
        warm = held.tile([P, 1], F32, name="warm")
        nc.scalar.activation(warm[:], warm_in[:], ACT.Sigmoid)
        two_list = load_list("two_list", two)
        offs_list = load_list("offs_list", offs)
        x_table = held.tile([P, TOKENS], U32, name="x_table")
        nc.sync.dma_start(x_table[:].bitcast(I32), x_words[0].rearrange("p c r -> p (c r)").bitcast(I32))
        w_rows = w1.rearrange("(p j) c -> p j c", j=PACK)
        w_raw = [held.tile([P, PACK, HALF], F32, name="w_raw%d" % h, tag="w_raw%d" % h, align_bytes=64) for h in range(2)]
        for h in range(2):
            nc.sync.dma_start(w_raw[h][:], w_rows[:, :, h * HALF : (h + 1) * HALF])
        k1_list = load_list("k1_list", k1)
        d_rows = d_scales[0].bitcast(I32).rearrange("(g e) c -> e g c", e=2)
        for e in range(2):
            nc.sync.dma_start(d_table_scales[e:P:16, :].bitcast(I32), d_rows[e])
        d_table = held.tile([P, CODEWORDS], U32, name="d_table")
        nc.sync.dma_start(d_table[:].bitcast(I32), d_words[0].rearrange("p c r -> p (c r)").bitcast(I32))
        n3_list = load_list("n3_list", n3)
        n4_list = load_list("n4_list", n4)
        gb_raw = held.tile([P, PACK], F32, name="gb_raw")
        nc.sync.dma_start(gb_raw[:], gb.rearrange("(p t) o -> p (t o)", t=PACK))
        ga_raw = held.tile([P, PACK], F32, name="ga_raw")
        nc.sync.dma_start(ga_raw[:], ga.rearrange("(p t) o -> p (t o)", t=PACK))
        n2_list = load_list("n2_list", n2)
        n1_list = load_list("n1_list", n1)
        n5_list = load_list("n5_list", n5)

        two_words = held.tile([P, N], U32, name="two_words", align_bytes=64)
        nc.vector.tensor_copy(two_words[:], x_table[:].indirect(two_list[:]))
        two_scales = held.tile([P, N], U8, name="two_scales", align_bytes=64)
        nc.vector.tensor_copy(two_scales[:], x_table_scales[:].indirect(two_list[:]))
        offs_scales = held.tile([P, N], U8, name="offs_scales", align_bytes=64)
        nc.vector.tensor_copy(offs_scales[:], x_table_scales[:].indirect(offs_list[:]))

        w_grouped = held.tile([P, PACK, P, PACK], BF16, name="w_grouped", tag="w_grouped", align_bytes=64)
        for h in range(2):
            nc.scalar.copy(
                w_grouped[:, :, h * P // 2 : (h + 1) * P // 2, :].rearrange("p t m j -> p m j t"),
                w_raw[h][:].rearrange("p j (m t) -> p m j t", t=PACK),
            )
        w_words = held.tile([P, PACK, P], U32, name="w_words", align_bytes=64)
        w_scales = held.tile([P, PACK, P], U8, name="w_scales", align_bytes=64)
        b_banks = []
        for t in range(PACK):
            nc.vector.quantize_mx(
                out=w_words[:, t, :].bitcast(FP8X4),
                scales=w_scales[:, t, :],
                in_=w_grouped[:, t, :, :].rearrange("p m j -> p (m j)"),
            )
            b_banks.append(product("b_bank%d" % t, t, w_words[:, t, :], w_scales[:, t, :], two_words[:], two_scales[:]))
        nc.scalar.copy(b[0][:, 0:N], b_banks[0][:])

        k1_scales = held.tile([P, N], U8, name="k1_scales", tag="w_raw1", align_bytes=64)
        nc.vector.tensor_copy(k1_scales[:], d_table_scales[:].indirect(k1_list[:]))
        picked_order = k1_scales[:].rearrange("p (m t) -> p m t", t=PACK)
        d_mm_scales = held.tile([P, N], U8, name="d_mm_scales", align_bytes=64)
        nc.vector.tensor_copy(d_mm_scales[:].rearrange("p (t m) -> p m t", t=PACK), picked_order)
        for e in range(2):
            nc.sync.dma_start(d_mm_scales[2 + e : P : 32, :].bitcast(I32), d_mm_scales[16 + e : P : 32, :].bitcast(I32))

        offs_words = held.tile([P, N], U32, name="offs_words", tag="w_grouped", align_bytes=64)
        nc.vector.tensor_copy(offs_words[:], x_table[:].indirect(offs_list[:]))
        k1_words = held.tile([P, N], U32, name="k1_words", tag="k1_words")
        nc.vector.tensor_copy(k1_words[:], d_table[:].indirect(k1_list[:]))
        d_mm_words = held.tile([P, PACK, P], U32, name="d_mm_words", align_bytes=64)
        nc.vector.tensor_copy(
            d_mm_words[:].rearrange("p t (c i) -> p c t i", i=4),
            k1_words[:].rearrange("p (c i t) -> p c t i", i=4, t=PACK),
        )
        for t in range(1, PACK):
            nc.vector.tensor_copy(b[t][:, 0:N], b_banks[t][:])

        gb_weight = held.tile([P, PACK], F32, name="gb_weight")
        nc.gpsimd.tensor_scalar(gb_weight[:], gb_raw[:], 0.75, 0.0, ALU.mult, ALU.add)
        ga_sixteenth = held.tile([P, PACK], F32, name="ga_sixteenth")
        nc.gpsimd.tensor_scalar(ga_sixteenth[:], ga_raw[:], SIXTEENTH, 0.0, ALU.mult, ALU.add)

        a = []
        a_banks = []
        for t in range(PACK):
            bank = product("a_bank%d" % t, PACK + t, d_mm_words[:, t, :], d_mm_scales[:, t * P : (t + 1) * P], offs_words[:], offs_scales[:])
            a_tile = held.tile([P, N], F32, name="a%d" % t)
            nc.vector.tensor_scalar_mul(a_tile[:], bank[:], SIXTEENTH)
            a.append(a_tile)
            a_banks.append(bank)

        def quantise(name, planes, width):
            grouped = held.tile([P, width, PACK], BF16, name=name + "_grouped", align_bytes=64)
            nc.vector.tensor_copy(
                grouped[:].rearrange("p (c i) t -> p c t i", i=4),
                planes[:].rearrange("p t (c i) -> p c t i", i=4),
            )
            words = held.tile([P, width], U32, name=name + "_words", align_bytes=64)
            scales = held.tile([P, width], U8, name=name + "_scales", align_bytes=64)
            nc.vector.quantize_mx(out=words[:].bitcast(FP8X4), scales=scales[:], in_=grouped[:].rearrange("p c t -> p (c t)"))
            return words, scales

        b_diffs = [
            held.tile([P, 2, 2, N], F32, name="b_diffs0", tag="k1_words"),
            held.tile([P, 2, 2, N], F32, name="b_diffs1", tag="w_grouped", align_bytes=64),
        ]
        z2_planes = held.tile([P, PACK, N], BF16, name="z2_planes")
        for t in range(PACK):
            b_n3 = ring.tile([P, N], F32, name="b_n3", bufs=PACK)
            b_n4 = ring.tile([P, N], F32, name="b_n4", bufs=PACK)
            nc.scalar.activation(b_n3[:], b[t][:].indirect(n3_list[:]), ACT.Copy)
            nc.scalar.activation(b_n4[:], b[t][:].indirect(n4_list[:]), ACT.Copy)
            diff3 = b_diffs[t // 2][:, t % 2, 0, :]
            diff4 = b_diffs[t // 2][:, t % 2, 1, :]
            nc.vector.tensor_tensor(diff3, b_banks[t][:], b_n3[:], ALU.subtract)
            nc.vector.tensor_tensor(diff4, b_banks[t][:], b_n4[:], ALU.subtract)
            if t < PACK - 1:
                diff3_weighted = ring.tile([P, N], F32, name="diff3_weighted")
                nc.gpsimd.tensor_scalar(diff3_weighted[:], diff3, gb_weight[:, t : t + 1], 0.0, ALU.mult, ALU.add)
                nc.gpsimd.tensor_tensor(z2_planes[:, t, :], diff3_weighted[:], diff4, ALU.mult)
            else:
                nc.vector.scalar_tensor_tensor(z2_planes[:, t, :], diff3, gb_weight[:, t : t + 1], diff4, ALU.mult, ALU.mult)
        z2_words, z2_scales = quantise("z2", z2_planes, N)

        def z_half(h):
            cols = slice(h * HALF, (h + 1) * HALF)
            planes = held.tile([P, PACK, HALF], BF16, name="z_planes%d" % h, tag="z_stage%d" % (h + 1))
            sig = held.tile([P, PACK, HALF], F32, name="sig%d" % h)
            a_n2 = held.tile([P, PACK, HALF], F32, name="a_n2_%d" % h)
            diff = held.tile([P, PACK, HALF], F32, name="diff_%d" % h, tag="z_stage%d" % h)
            pull = held.tile([P, PACK, HALF], F32, name="pull%d" % h)
            for t in range(PACK):
                nc.scalar.activation(a_n2[:, t, :], a[t][:].indirect(entries(n2_list, h * HALF, HALF)), ACT.Copy)
            for t in range(PACK):
                nc.scalar.activation(sig[:, t, :], a[t][:].indirect(entries(n1_list, h * HALF, HALF)), ACT.Sigmoid)
            for t in range(PACK):
                nc.vector.scalar_tensor_tensor(diff[:, t, :], a_banks[t][:, cols], SIXTEENTH, a_n2[:, t, :], ALU.mult, ALU.subtract)
            for t in range(PACK):
                nc.vector.scalar_tensor_tensor(pull[:, t, :], diff[:, t, :], ga_raw[:, t : t + 1], sig[:, t, :], ALU.mult, ALU.mult)
            for t in range(PACK):
                nc.vector.scalar_tensor_tensor(planes[:, t, :], a_banks[t][:, cols], ga_sixteenth[:, t : t + 1], pull[:, t, :], ALU.mult, ALU.subtract)
            return quantise("z%d" % h, planes, HALF)

        z_halves = [z_half(h) for h in range(2)]

        for r in range(PACK):
            z_words, z_scales = z_halves[r // 2]
            z_cols = slice(r % 2 * P, (r % 2 + 1) * P)
            bank = product("s_bank%d" % r, r, z_words[:, z_cols], z_scales[:, z_cols], z2_words[:], z2_scales[:])
            nc.scalar.activation(s[r][:, 0:N], bank[:], ACT.Copy, scale=SIXTEENTH)
            for h in range(2):
                cols = slice(h * HALF, (h + 1) * HALF)
                members = ring.tile([P, HALF, MEMBERS], F32, name="members", bufs=4)
                nc.scalar.activation(
                    members[:].rearrange("p v m -> p (v m)"),
                    s[r][:].indirect(entries(n5_list, h * HALF * MEMBERS, HALF * MEMBERS)),
                    ACT.Copy,
                )
                high_pair = ring.tile([P, HALF, 2], F32, name="high_pair")
                low_pair = ring.tile([P, HALF, 2], F32, name="low_pair")
                largest = ring.tile([P, HALF], F32, name="largest")
                smallest = ring.tile([P, HALF], F32, name="smallest")
                capped = ring.tile([P, HALF], F32, name="capped")
                result = ring.tile([P, HALF], F32, name="result", bufs=4)
                nc.vector.tensor_tensor(high_pair[:], members[:, :, 0:2], members[:, :, 2:4], ALU.max)
                nc.vector.tensor_tensor(low_pair[:], members[:, :, 0:2], members[:, :, 2:4], ALU.min)
                nc.vector.tensor_tensor(largest[:], high_pair[:, :, 0], high_pair[:, :, 1], ALU.max)
                nc.vector.tensor_tensor(smallest[:], low_pair[:, :, 0], low_pair[:, :, 1], ALU.min)
                nc.vector.scalar_tensor_tensor(capped[:], s[r][:, cols], 1.5, largest[:], ALU.mult, ALU.min)
                nc.vector.tensor_tensor(result[:], capped[:], smallest[:], ALU.max)
                nc.sync.dma_start(out[r * P : (r + 1) * P, cols], result[:])
